import numpy as np
import ml_dtypes


def mxq(x, axis, fmt="e4m3"):
    dtype, down = {"e4m3": (ml_dtypes.float8_e4m3fn, 7), "e5m2": (ml_dtypes.float8_e5m2, 14)}[fmt]
    v = np.moveaxis(np.asarray(x, np.float32).astype(ml_dtypes.bfloat16).astype(np.float64), axis, -1)
    blocks = v.reshape(v.shape[:-1] + (-1, 32))
    amax = np.abs(blocks).max(-1, keepdims=True)
    byte = np.maximum(np.where(amax > 0, np.frexp(amax)[1] - 1 + 127, 0) - down, 1)
    scale = np.exp2(byte - 127.0)
    codes = (blocks / scale).astype(np.float32).astype(dtype).astype(np.float64)
    return np.moveaxis((codes * scale).reshape(v.shape), -1, axis)


WIDE = False


def mx_kscale(k):
    if not WIDE:
        return np.ones(k)
    levels = np.array([10, -10, 5, -5, 0])
    if k % 512:
        return np.exp2(np.random.permutation(np.resize(levels, k // 32))).repeat(32)
    a = np.empty((k // 512, 16))
    for p in range(k // 512):
        a[p, :8] = np.random.permutation(np.resize(levels, 8))
        for g in range(8):
            far = levels[np.abs(levels - a[p, g]) >= 10]
            a[p, g + 8] = far[np.random.randint(len(far))]
    return np.exp2(a.ravel()).repeat(32)


def f64(x):
    return np.asarray(x).astype(np.float64)


def striped(idx):
    return np.tile(idx.reshape(-1, 16).T, (8, 1)).astype(np.uint16)


def unstriped(offs):
    return offs[:16].T.reshape(-1).astype(np.int64)


def pack_weight(w):
    k, n = w.shape
    w = f64(np.asarray(w, np.float32).astype(ml_dtypes.bfloat16)).reshape(k // 32, 32, n)
    amax = np.abs(w).max(1)
    byte = np.clip(np.where(amax > 0, np.frexp(amax)[1] - 1 + 127 - 7, 1), 1, 254)
    scaled = (w * np.exp2(127.0 - byte)[:, None, :]).reshape(k, n).astype(np.float32)
    words = np.ascontiguousarray(scaled.reshape(k // 512, 128, 4, n).transpose(0, 1, 3, 2)).astype(ml_dtypes.float8_e4m3fn).view(np.uint8)
    return words, np.ascontiguousarray(byte.astype(np.uint8).reshape(k // 512, 16, n))


def unpack_weight(words, scales):
    g, p, n, _ = words.shape
    vals = np.ascontiguousarray(words).view(ml_dtypes.float8_e4m3fn).astype(np.float64) * np.repeat(np.exp2(scales.astype(np.float64) - 127.0), 8, axis=1)[..., None]
    return vals.transpose(0, 1, 3, 2).reshape(g * 512, n)


def relu(v):
    return np.maximum(v, 0.0)


K, T, S, V, U = 1024, 1024, 512, 256, 256


def setup_inputs():
    n = np.random.standard_normal
    s = mx_kscale(K)[:, None]
    packed_xT = pack_weight(n((K, T)) * s)
    return {
        "x_words": packed_xT[0],
        "x_scales": packed_xT[1],
        "hT": (n((K, V)) / np.sqrt(K) / s).astype(np.float32),
        "gT": (n((K, V)) / np.sqrt(K) / s).astype(np.float32),
        "offs": striped(np.random.permutation(T)[:S]),
        "tree1": striped(np.random.randint(0, S, U)),
        "tree2": striped(np.random.randint(0, S, U)),
        "tree3": striped(np.random.randint(0, S, U)),
    }


def reference(x_words, x_scales, hT, gT, offs, tree1, tree2, tree3):
    hTq = mxq(f64(hT), 0, "e4m3")
    xq = unpack_weight(x_words, x_scales)[:, unstriped(offs)]
    y = hTq.T @ xq
    ee = np.exp(y)
    se = np.log(ee.sum(axis=1, keepdims=True))
    ly = y - se
    gTq = mxq(f64(gT), 0, "e4m3")
    z = gTq.T @ xq
    a = np.exp(z)
    sa = np.log(a.sum(axis=1, keepdims=True))
    lz = z - sa
    dd = ly - lz
    gg = -1.0 * relu(-1.0 * dd)
    return gg[:, unstriped(tree1)] + gg[:, unstriped(tree2)] + gg[:, unstriped(tree3)]

@@ -1,0 +1,197 @@
+import math
+from contextlib import ExitStack
+
+import concourse.mybir as mybir
+
+K, T, S, V, U = 1024, 1024, 512, 256, 256
+FLOPS = 2 * 2 * K * S * V
+
+F32 = mybir.dt.float32
+BF16 = mybir.dt.bfloat16
+I32 = mybir.dt.int32
+U32 = mybir.dt.uint32
+U16 = mybir.dt.uint16
+U8 = mybir.dt.uint8
+FP8X4 = mybir.dt.float8_e4m3fn_x4
+ALU = mybir.AluOpType
+ACT = mybir.ActivationFunctionType
+
+P = 128
+PASSES = 2
+BLOCKS = 2
+NODES = 96
+LOG_STEP = -1.0
+LOG_FIRST_NODE = 3.25
+
+
+def tile_picked_yacc_log_p_kernel(tc, x_words, x_scales, hT, gT, offs, tree1, tree2, tree3, out):
+    nc = tc.nc
+    with ExitStack() as ctx:
+        keep = ctx.enter_context(tc.tile_pool(name="keep", bufs=1))
+        psum = ctx.enter_context(tc.psum_pool(name="psum", bufs=1))
+
+        scale_table = keep.tile([P, T], U8, name="scale_table")
+        nc.gpsimd.memset(scale_table[:].bitcast(I32), 0)
+
+        offs_sb = keep.tile([P, S // 16], U16, name="offs_sb")
+        nc.sync.dma_start(offs_sb[:], offs)
+        for q in range(4):
+            nc.sync.dma_start(
+                scale_table[32 * q : 32 * q + 8, :].bitcast(I32),
+                x_scales[:, 4 * q : 4 * q + 4, :].bitcast(I32),
+            )
+
+        counts = keep.tile([P, NODES], F32, name="counts")
+        nc.gpsimd.iota(counts[:], [[1, NODES]], base=0, channel_multiplier=0, allow_small_or_imprecise_dtypes=True)
+        nodes = keep.tile([P, NODES], F32, name="nodes")
+        nc.scalar.activation(nodes[:], counts[:], ACT.Exp, bias=LOG_FIRST_NODE, scale=-math.exp(LOG_STEP))
+        neg_nodes = keep.tile([P, NODES], F32, name="neg_nodes")
+        nc.scalar.activation(neg_nodes[:], nodes[:], ACT.Copy, scale=-1.0)
+
+        def load_words(o):
+            table = keep.tile([P, T], U32, name=f"word_table{o}")
+            nc.sync.dma_start(table[:].bitcast(I32), x_words[o].rearrange("p n t -> p (n t)").bitcast(I32))
+            return table
+
+        def load_rows(src, name, o, c0, width):
+            raw = keep.tile([P, 4, width], F32, name=f"raw_{name}", tag=f"raw_{name}")
+            nc.sync.dma_start(raw[:], src[512 * o : 512 * (o + 1), :].rearrange("(p j) c -> p j c", j=4)[:, :, c0 : c0 + width])
+            return raw
+
+        def scalar_copy(dst, src):
+            nc.scalar.activation(dst, src, ACT.Copy)
+
+        def weave_into(engine_copy, woven, raw):
+            engine_copy(woven.rearrange("p (c i) j -> p c j i", i=4), raw.rearrange("p j (c i) -> p c j i", i=4))
+
+        def weave(engine_copy, raw, c0, width, name):
+            woven = keep.tile([P, width, 4], BF16, name=f"woven_{name}", tag=f"woven_{name}", align_bytes=64)
+            engine_copy(
+                woven[:].rearrange("p (c i) j -> p c j i", i=4),
+                raw[:, :, c0 : c0 + width].rearrange("p j (c i) -> p c j i", i=4),
+            )
+            return woven
+
+        def quantise(woven, width, name):
+            codes = keep.tile([P, width], U32, name=f"codes_{name}", align_bytes=64)
+            scales = keep.tile([P, width], U8, name=f"scales_{name}", align_bytes=64)
+            nc.vector.quantize_mx(codes[:].bitcast(FP8X4), scales[:], woven[:].rearrange("p c j -> p (c j)"))
+            return codes, scales
+
+        table0 = load_words(0)
+        raw_ha = load_rows(hT, "ha", 0, 0, V)
+        table1 = load_words(1)
+        raw_hb = load_rows(hT, "hb", 1, 0, V)
+        raw_ga = load_rows(gT, "ga", 0, 0, V)
+        raw_gb0 = load_rows(gT, "gb0", 1, 0, P)
+        raw_gb1 = load_rows(gT, "gb1", 1, P, P)
+        trees = []
+        for n, tree in enumerate((tree1, tree2, tree3)):
+            tree_sb = keep.tile([P, U // 16], U16, name=f"tree_sb{n}")
+            nc.sync.dma_start(tree_sb[:], tree)
+            trees.append(tree_sb)
+
+        picked_words = [keep.tile([P, S], U32, name="picked_words0", align_bytes=64)]
+        picked_scales = keep.tile([P, S], U8, name="picked_scales", align_bytes=64)
+
+        def mx_pass(acc, o, codes, scales):
+            nc.tensor.matmul_mx(
+                acc[:],
+                lhsT=codes.bitcast(FP8X4),
+                lhsT_scale=scales,
+                rhs=picked_words[o][:].bitcast(FP8X4),
+                rhs_scale=picked_scales[4 * o :, :],
+                start=(o == 0),
+                stop=(o == PASSES - 1),
+            )
+
+
+        def column(name):
+            return keep.tile([P, 1], F32, name=name)
+
+        def negate(acc, name, tag):
+            neg = keep.tile([P, S], F32, name=f"neg_{name}", tag=tag, align_bytes=64)
+            neg_max = column(f"neg_max_{name}")
+            nc.vector.tensor_scalar(neg[:], acc[:], -1.0, None, ALU.mult, ALU.min, accum_out=neg_max[:])
+            return neg, neg_max
+
+        def exp_sum(neg, neg_max, name):
+            total = column(f"total_{name}")
+            nc.scalar.activation(unused[:], neg[:], ACT.Exp, bias=neg_max[:], scale=-1.0, accum_out=total[:])
+            return total
+
+        def neg_log(total, name):
+            res = column(f"neg_log_{name}")
+            nc.scalar.activation(unused[:, 0:NODES], neg_nodes[:], ACT.Exp, bias=LOG_STEP, scale=total[:], accum_out=res[:])
+            return res
+
+        def combine(a, scale, b, name):
+            res = column(name)
+            nc.scalar.activation(res[:], a[:], ACT.Identity, bias=b[:], scale=scale)
+            return res
+
+        def paths(b, gg):
+            one = keep.tile([P, U], F32, name=f"one{b}")
+            two = keep.tile([P, U], F32, name=f"two{b}")
+            three = keep.tile([P, U], F32, name=f"three{b}")
+            nc.vector.tensor_copy(one[:], gg[:].indirect(trees[0][:]))
+            nc.vector.tensor_tensor(two[:], gg[:].indirect(trees[1][:]), one[:], ALU.add)
+            nc.vector.tensor_tensor(three[:], gg[:].indirect(trees[2][:]), two[:], ALU.add)
+            nc.sync.dma_start(out[P * b : P * (b + 1), :], three[:])
+
+        y = [psum.tile([P, S], F32, name=f"y{b}") for b in range(BLOCKS)]
+        z = [psum.tile([P, S], F32, name=f"z{b}") for b in range(BLOCKS)]
+        cols = [slice(P * b, P * (b + 1)) for b in range(BLOCKS)]
+
+        nc.vector.tensor_copy(picked_scales[:], scale_table[:].indirect(offs_sb[:]))
+        nc.vector.tensor_copy(picked_words[0][:], table0[:].indirect(offs_sb[:]))
+        woven_ha = weave(scalar_copy, raw_ha, 0, V, "ha")
+        codes, scales = quantise(woven_ha, V, "ha")
+        for b in range(BLOCKS):
+            mx_pass(y[b], 0, codes[:, cols[b]], scales[:, cols[b]])
+        picked_words.append(keep.tile([P, S], U32, name="picked_words1", tag="woven_ha", align_bytes=64))
+        nc.vector.tensor_copy(picked_words[1][:], table1[:].indirect(offs_sb[:]))
+        woven_hb1 = weave(scalar_copy, raw_hb, P, P, "hb1")
+        woven_hb0 = weave(nc.vector.tensor_copy, raw_hb, 0, P, "hb0")
+        codes1, scales1 = quantise(woven_hb1, P, "hb1")
+        codes0, scales0 = quantise(woven_hb0, P, "hb0")
+        mx_pass(y[0], 1, codes0[:], scales0[:])
+        mx_pass(y[1], 1, codes1[:], scales1[:])
+        woven_ga0 = weave(scalar_copy, raw_ga, 0, P, "ga0")
+        woven_g1 = keep.tile([P, V, 4], BF16, name="woven_g1", tag="woven_g1", align_bytes=64)
+        weave_into(scalar_copy, woven_g1[:, 0:P, :], raw_ga[:, :, P:V])
+        woven_gb0 = weave(nc.vector.tensor_copy, raw_gb0, 0, P, "gb0")
+        codes, scales = quantise(woven_ga0, P, "ga0")
+        mx_pass(z[0], 0, codes[:], scales[:])
+        codes, scales = quantise(woven_gb0, P, "gb0")
+        mx_pass(z[0], 1, codes[:], scales[:])
+        weave_into(scalar_copy, woven_g1[:, P:V, :], raw_gb1[:])
+        unused = keep.tile([P, S], F32, name="unused", tag="raw_gb1")
+        ny0, nmy0 = negate(y[0], "y0", "woven_gb0")
+        codes, scales = quantise(woven_g1, V, "g1")
+        for o in range(PASSES):
+            mx_pass(z[1], o, codes[:, cols[o]], scales[:, cols[o]])
+        nz0, nmz0 = negate(z[0], "z0", "neg_z0")
+        ny1, nmy1 = negate(y[1], "y1", "woven_g1")
+        ay0 = neg_log(exp_sum(ny0, nmy0, "y0"), "y0")
+        sz0 = exp_sum(nz0, nmz0, "z0")
+        wy0 = combine(ay0, 1.0, nmy0, "wy0")
+        c0 = combine(wy0, -1.0, neg_log(sz0, "z0"), "c0")
+        gg = [keep.tile([P, S], F32, name=f"gg{b}") for b in range(BLOCKS)]
+        diff0 = keep.tile([P, S], F32, name="diff0", tag="diff")
+        nc.vector.scalar_tensor_tensor(diff0[:], nz0[:], nmz0[:], ny0[:], ALU.subtract, ALU.subtract)
+        nz1, nmz1 = negate(z[1], "z1", "neg_z1")
+        sy1 = exp_sum(ny1, nmy1, "y1")
+        sz1 = exp_sum(nz1, nmz1, "z1")
+        ay1 = neg_log(sy1, "y1")
+        az1 = neg_log(sz1, "z1")
+        wy1 = combine(ay1, 1.0, nmy1, "wy1")
+        c1 = combine(wy1, -1.0, az1, "c1")
+        nc.vector.tensor_scalar(gg[0][:], diff0[:], c0[:], 0.0, ALU.subtract, ALU.min)
+        diff1 = keep.tile([P, S], F32, name="diff1", tag="diff")
+        nc.vector.scalar_tensor_tensor(diff1[:], nz1[:], nmz1[:], ny1[:], ALU.subtract, ALU.subtract)
+        paths(0, gg[0])
+        rejected = keep.tile([P, S], F32, name="rejected")
+        nc.scalar.activation(rejected[:], diff1[:], ACT.Relu, bias=c1[:], scale=-1.0)
+        nc.scalar.activation(gg[1][:], rejected[:], ACT.Copy, scale=-1.0)
+        paths(1, gg[1])

@@ -49,7 +49,7 @@ def tile_picked_yacc_log_p_kernel(tc, x_words, x_scales, hT, gT, offs, tree1, tr
         nc.scalar.activation(neg_nodes[:], nodes[:], ACT.Copy, scale=-1.0)
 
         def load_words(o):
-            table = keep.tile([P, T], U32, name=f"word_table{o}")
+            table = keep.tile([P, T], U32, name=f"word_table{o}", tag=f"word_table{o}", align_bytes=64)
             nc.sync.dma_start(table[:].bitcast(I32), x_words[o].rearrange("p n t -> p (n t)").bitcast(I32))
             return table
 
@@ -64,8 +64,8 @@ def tile_picked_yacc_log_p_kernel(tc, x_words, x_scales, hT, gT, offs, tree1, tr
         def weave_into(engine_copy, woven, raw):
             engine_copy(woven.rearrange("p (c i) j -> p c j i", i=4), raw.rearrange("p j (c i) -> p c j i", i=4))
 
-        def weave(engine_copy, raw, c0, width, name):
-            woven = keep.tile([P, width, 4], BF16, name=f"woven_{name}", tag=f"woven_{name}", align_bytes=64)
+        def weave(engine_copy, raw, c0, width, name, tag=None):
+            woven = keep.tile([P, width, 4], BF16, name=f"woven_{name}", tag=tag or f"woven_{name}", align_bytes=64)
             engine_copy(
                 woven[:].rearrange("p (c i) j -> p c j i", i=4),
                 raw[:, :, c0 : c0 + width].rearrange("p j (c i) -> p c j i", i=4),
@@ -131,67 +131,71 @@ def tile_picked_yacc_log_p_kernel(tc, x_words, x_scales, hT, gT, offs, tree1, tr
             return res
 
         def paths(b, gg):
-            one = keep.tile([P, U], F32, name=f"one{b}")
-            two = keep.tile([P, U], F32, name=f"two{b}")
-            three = keep.tile([P, U], F32, name=f"three{b}")
-            nc.vector.tensor_copy(one[:], gg[:].indirect(trees[0][:]))
-            nc.vector.tensor_tensor(two[:], gg[:].indirect(trees[1][:]), one[:], ALU.add)
-            nc.vector.tensor_tensor(three[:], gg[:].indirect(trees[2][:]), two[:], ALU.add)
-            nc.sync.dma_start(out[P * b : P * (b + 1), :], three[:])
+            sums = [keep.tile([P, U], F32, name=f"sum{b}{n}") for n in range(3)]
+            halves = [(slice(P * h, P * (h + 1)), slice(8 * h, 8 * (h + 1))) for h in range(2)]
+            for part, entries in halves:
+                nc.vector.tensor_copy(sums[0][:, part], gg[:].indirect(trees[0][:, entries]))
+            for n in (1, 2):
+                for part, entries in halves:
+                    nc.vector.tensor_tensor(sums[n][:, part], gg[:].indirect(trees[n][:, entries]), sums[n - 1][:, part], ALU.add)
+            for part, entries in halves:
+                nc.sync.dma_start(out[P * b : P * (b + 1), part], sums[2][:, part])
 
         y = [psum.tile([P, S], F32, name=f"y{b}") for b in range(BLOCKS)]
         z = [psum.tile([P, S], F32, name=f"z{b}") for b in range(BLOCKS)]
         cols = [slice(P * b, P * (b + 1)) for b in range(BLOCKS)]
 
-        nc.vector.tensor_copy(picked_scales[:], scale_table[:].indirect(offs_sb[:]))
         nc.vector.tensor_copy(picked_words[0][:], table0[:].indirect(offs_sb[:]))
-        woven_ha = weave(scalar_copy, raw_ha, 0, V, "ha")
+        nc.vector.tensor_copy(picked_scales[:], scale_table[:].indirect(offs_sb[:]))
+        woven_ha = keep.tile([P, V, 4], BF16, name="woven_ha", tag="woven_ha", align_bytes=64)
+        weave_into(nc.vector.tensor_copy, woven_ha[:, 0:P, :], raw_ha[:, :, 0:P])
+        weave_into(scalar_copy, woven_ha[:, P:V, :], raw_ha[:, :, P:V])
         codes, scales = quantise(woven_ha, V, "ha")
         for b in range(BLOCKS):
             mx_pass(y[b], 0, codes[:, cols[b]], scales[:, cols[b]])
         picked_words.append(keep.tile([P, S], U32, name="picked_words1", tag="woven_ha", align_bytes=64))
         nc.vector.tensor_copy(picked_words[1][:], table1[:].indirect(offs_sb[:]))
-        woven_hb1 = weave(scalar_copy, raw_hb, P, P, "hb1")
-        woven_hb0 = weave(nc.vector.tensor_copy, raw_hb, 0, P, "hb0")
-        codes1, scales1 = quantise(woven_hb1, P, "hb1")
-        codes0, scales0 = quantise(woven_hb0, P, "hb0")
-        mx_pass(y[0], 1, codes0[:], scales0[:])
-        mx_pass(y[1], 1, codes1[:], scales1[:])
-        woven_ga0 = weave(scalar_copy, raw_ga, 0, P, "ga0")
-        woven_g1 = keep.tile([P, V, 4], BF16, name="woven_g1", tag="woven_g1", align_bytes=64)
-        weave_into(scalar_copy, woven_g1[:, 0:P, :], raw_ga[:, :, P:V])
-        woven_gb0 = weave(nc.vector.tensor_copy, raw_gb0, 0, P, "gb0")
-        codes, scales = quantise(woven_ga0, P, "ga0")
-        mx_pass(z[0], 0, codes[:], scales[:])
-        codes, scales = quantise(woven_gb0, P, "gb0")
-        mx_pass(z[0], 1, codes[:], scales[:])
-        weave_into(scalar_copy, woven_g1[:, P:V, :], raw_gb1[:])
+        woven_hb = keep.tile([P, V, 4], BF16, name="woven_hb", tag="word_table1", align_bytes=64)
+        weave_into(nc.vector.tensor_copy, woven_hb[:, 0:P, :], raw_hb[:, :, 0:P])
+        weave_into(scalar_copy, woven_hb[:, P:V, :], raw_hb[:, :, P:V])
+        codes, scales = quantise(woven_hb, V, "hb")
+        for b in range(BLOCKS):
+            mx_pass(y[b], 1, codes[:, cols[b]], scales[:, cols[b]])
+        woven_g = []
+        for b, raw_gb in enumerate((raw_gb0, raw_gb1)):
+            woven = keep.tile([P, V, 4], BF16, name=f"woven_g{b}", tag=f"woven_g{b}", align_bytes=64)
+            weave_into(scalar_copy, woven[:, 0:P, :], raw_ga[:, :, cols[b]])
+            weave_into(scalar_copy, woven[:, P:V, :], raw_gb[:])
+            woven_g.append(woven)
         unused = keep.tile([P, S], F32, name="unused", tag="raw_gb1")
-        ny0, nmy0 = negate(y[0], "y0", "woven_gb0")
-        codes, scales = quantise(woven_g1, V, "g1")
-        for o in range(PASSES):
-            mx_pass(z[1], o, codes[:, cols[o]], scales[:, cols[o]])
-        nz0, nmz0 = negate(z[0], "z0", "neg_z0")
-        ny1, nmy1 = negate(y[1], "y1", "woven_g1")
+
+        def small_product(b):
+            codes, scales = quantise(woven_g[b], V, f"g{b}")
+            for o in range(PASSES):
+                mx_pass(z[b], o, codes[:, cols[o]], scales[:, cols[o]])
+
+        ny0, nmy0 = negate(y[0], "y0", "neg_y0")
+        small_product(0)
+        ny1, nmy1 = negate(y[1], "y1", "woven_g0")
+        small_product(1)
+        nz0, nmz0 = negate(z[0], "z0", "woven_g1")
         ay0 = neg_log(exp_sum(ny0, nmy0, "y0"), "y0")
-        sz0 = exp_sum(nz0, nmz0, "z0")
-        wy0 = combine(ay0, 1.0, nmy0, "wy0")
-        c0 = combine(wy0, -1.0, neg_log(sz0, "z0"), "c0")
-        gg = [keep.tile([P, S], F32, name=f"gg{b}") for b in range(BLOCKS)]
-        diff0 = keep.tile([P, S], F32, name="diff0", tag="diff")
-        nc.vector.scalar_tensor_tensor(diff0[:], nz0[:], nmz0[:], ny0[:], ALU.subtract, ALU.subtract)
-        nz1, nmz1 = negate(z[1], "z1", "neg_z1")
         sy1 = exp_sum(ny1, nmy1, "y1")
+        wy0 = combine(ay0, 1.0, nmy0, "wy0")
+        c0 = combine(wy0, -1.0, neg_log(exp_sum(nz0, nmz0, "z0"), "z0"), "c0")
+        gg = [keep.tile([P, S], F32, name=f"gg{b}") for b in range(BLOCKS)]
+        diffs = [keep.tile([P, S], F32, name=f"diff{b}") for b in range(BLOCKS)]
+        nc.vector.scalar_tensor_tensor(diffs[0][:], nz0[:], nmz0[:], ny0[:], ALU.subtract, ALU.subtract)
+        nz1, nmz1 = negate(z[1], "z1", "neg_z1")
+        nc.vector.scalar_tensor_tensor(diffs[1][:], nz1[:], nmz1[:], ny1[:], ALU.subtract, ALU.subtract)
         sz1 = exp_sum(nz1, nmz1, "z1")
         ay1 = neg_log(sy1, "y1")
         az1 = neg_log(sz1, "z1")
         wy1 = combine(ay1, 1.0, nmy1, "wy1")
         c1 = combine(wy1, -1.0, az1, "c1")
-        nc.vector.tensor_scalar(gg[0][:], diff0[:], c0[:], 0.0, ALU.subtract, ALU.min)
-        diff1 = keep.tile([P, S], F32, name="diff1", tag="diff")
-        nc.vector.scalar_tensor_tensor(diff1[:], nz1[:], nmz1[:], ny1[:], ALU.subtract, ALU.subtract)
+        nc.vector.tensor_scalar(gg[0][:], diffs[0][:], c0[:], 0.0, ALU.subtract, ALU.min)
         paths(0, gg[0])
         rejected = keep.tile([P, S], F32, name="rejected")
-        nc.scalar.activation(rejected[:], diff1[:], ACT.Relu, bias=c1[:], scale=-1.0)
+        nc.scalar.activation(rejected[:], diffs[1][:], ACT.Relu, bias=c1[:], scale=-1.0)
         nc.scalar.activation(gg[1][:], rejected[:], ACT.Copy, scale=-1.0)
         paths(1, gg[1])

@@ -75,7 +75,7 @@ def tile_picked_yacc_log_p_kernel(tc, x_words, x_scales, hT, gT, offs, tree1, tr
         def quantise(woven, width, name):
             codes = keep.tile([P, width], U32, name=f"codes_{name}", align_bytes=64)
             scales = keep.tile([P, width], U8, name=f"scales_{name}", align_bytes=64)
-            nc.vector.quantize_mx(codes[:].bitcast(FP8X4), scales[:], woven[:].rearrange("p c j -> p (c j)"))
+            nc.vector.quantize_mx(codes[:].bitcast(FP8X4), scales[:], woven.rearrange("p c j -> p (c j)"))
             return codes, scales
 
         table0 = load_words(0)
@@ -83,13 +83,12 @@ def tile_picked_yacc_log_p_kernel(tc, x_words, x_scales, hT, gT, offs, tree1, tr
         table1 = load_words(1)
         raw_hb = load_rows(hT, "hb", 1, 0, V)
         raw_ga = load_rows(gT, "ga", 0, 0, V)
-        raw_gb0 = load_rows(gT, "gb0", 1, 0, P)
-        raw_gb1 = load_rows(gT, "gb1", 1, P, P)
         trees = []
         for n, tree in enumerate((tree1, tree2, tree3)):
             tree_sb = keep.tile([P, U // 16], U16, name=f"tree_sb{n}")
             nc.sync.dma_start(tree_sb[:], tree)
             trees.append(tree_sb)
+        raw_gb = load_rows(gT, "gb", 1, 0, V)
 
         picked_words = [keep.tile([P, S], U32, name="picked_words0", align_bytes=64)]
         picked_scales = keep.tile([P, S], U8, name="picked_scales", align_bytes=64)
@@ -150,7 +149,7 @@ def tile_picked_yacc_log_p_kernel(tc, x_words, x_scales, hT, gT, offs, tree1, tr
         woven_ha = keep.tile([P, V, 4], BF16, name="woven_ha", tag="woven_ha", align_bytes=64)
         weave_into(nc.vector.tensor_copy, woven_ha[:, 0:P, :], raw_ha[:, :, 0:P])
         weave_into(scalar_copy, woven_ha[:, P:V, :], raw_ha[:, :, P:V])
-        codes, scales = quantise(woven_ha, V, "ha")
+        codes, scales = quantise(woven_ha[:], V, "ha")
         for b in range(BLOCKS):
             mx_pass(y[b], 0, codes[:, cols[b]], scales[:, cols[b]])
         picked_words.append(keep.tile([P, S], U32, name="picked_words1", tag="woven_ha", align_bytes=64))
@@ -158,41 +157,35 @@ def tile_picked_yacc_log_p_kernel(tc, x_words, x_scales, hT, gT, offs, tree1, tr
         woven_hb = keep.tile([P, V, 4], BF16, name="woven_hb", tag="word_table1", align_bytes=64)
         weave_into(nc.vector.tensor_copy, woven_hb[:, 0:P, :], raw_hb[:, :, 0:P])
         weave_into(scalar_copy, woven_hb[:, P:V, :], raw_hb[:, :, P:V])
-        codes, scales = quantise(woven_hb, V, "hb")
+        hb_quantised = {b: quantise(woven_hb[:, cols[b], :], P, f"hb{b}") for b in (1, 0)}
         for b in range(BLOCKS):
-            mx_pass(y[b], 1, codes[:, cols[b]], scales[:, cols[b]])
-        woven_g = []
-        for b, raw_gb in enumerate((raw_gb0, raw_gb1)):
-            woven = keep.tile([P, V, 4], BF16, name=f"woven_g{b}", tag=f"woven_g{b}", align_bytes=64)
-            weave_into(scalar_copy, woven[:, 0:P, :], raw_ga[:, :, cols[b]])
-            weave_into(scalar_copy, woven[:, P:V, :], raw_gb[:])
-            woven_g.append(woven)
-        unused = keep.tile([P, S], F32, name="unused", tag="raw_gb1")
-
-        def small_product(b):
-            codes, scales = quantise(woven_g[b], V, f"g{b}")
-            for o in range(PASSES):
-                mx_pass(z[b], o, codes[:, cols[o]], scales[:, cols[o]])
-
+            mx_pass(y[b], 1, hb_quantised[b][0][:], hb_quantised[b][1][:])
+        woven_ga = [weave(scalar_copy, raw_ga, P * b, P, f"ga{b}") for b in range(BLOCKS)]
         ny0, nmy0 = negate(y[0], "y0", "neg_y0")
-        small_product(0)
-        ny1, nmy1 = negate(y[1], "y1", "woven_g0")
-        small_product(1)
-        nz0, nmz0 = negate(z[0], "z0", "woven_g1")
+        for b in range(BLOCKS):
+            codes, scales = quantise(woven_ga[b][:], P, f"ga{b}")
+            mx_pass(z[b], 0, codes[:], scales[:])
+        woven_gb = [weave(nc.vector.tensor_copy, raw_gb, 0, P, "gb0"), weave(scalar_copy, raw_gb, P, P, "gb1")]
+        gb_quantised = {b: quantise(woven_gb[b][:], P, f"gb{b}") for b in (1, 0)}
+        for b in range(BLOCKS):
+            mx_pass(z[b], 1, gb_quantised[b][0][:], gb_quantised[b][1][:])
+        unused = keep.tile([P, S], F32, name="unused", tag="raw_gb")
+        ny1, nmy1 = negate(y[1], "y1", "woven_gb0")
+        nz0, nmz0 = negate(z[0], "z0", "neg_z0")
         ay0 = neg_log(exp_sum(ny0, nmy0, "y0"), "y0")
         sy1 = exp_sum(ny1, nmy1, "y1")
         wy0 = combine(ay0, 1.0, nmy0, "wy0")
-        c0 = combine(wy0, -1.0, neg_log(exp_sum(nz0, nmz0, "z0"), "z0"), "c0")
+        sz0 = exp_sum(nz0, nmz0, "z0")
+        ay1 = neg_log(sy1, "y1")
+        c0 = combine(wy0, -1.0, neg_log(sz0, "z0"), "c0")
         gg = [keep.tile([P, S], F32, name=f"gg{b}") for b in range(BLOCKS)]
         diffs = [keep.tile([P, S], F32, name=f"diff{b}") for b in range(BLOCKS)]
-        nc.vector.scalar_tensor_tensor(diffs[0][:], nz0[:], nmz0[:], ny0[:], ALU.subtract, ALU.subtract)
         nz1, nmz1 = negate(z[1], "z1", "neg_z1")
+        nc.vector.scalar_tensor_tensor(diffs[0][:], nz0[:], nmz0[:], ny0[:], ALU.subtract, ALU.subtract)
         nc.vector.scalar_tensor_tensor(diffs[1][:], nz1[:], nmz1[:], ny1[:], ALU.subtract, ALU.subtract)
         sz1 = exp_sum(nz1, nmz1, "z1")
-        ay1 = neg_log(sy1, "y1")
-        az1 = neg_log(sz1, "z1")
         wy1 = combine(ay1, 1.0, nmy1, "wy1")
-        c1 = combine(wy1, -1.0, az1, "c1")
+        c1 = combine(wy1, -1.0, neg_log(sz1, "z1"), "c1")
         nc.vector.tensor_scalar(gg[0][:], diffs[0][:], c0[:], 0.0, ALU.subtract, ALU.min)
         paths(0, gg[0])
         rejected = keep.tile([P, S], F32, name="rejected")

import math
from contextlib import ExitStack

import concourse.mybir as mybir

K, T, S, V, U = 1024, 1024, 512, 256, 256
FLOPS = 2 * 2 * K * S * V

F32 = mybir.dt.float32
BF16 = mybir.dt.bfloat16
I32 = mybir.dt.int32
U32 = mybir.dt.uint32
U16 = mybir.dt.uint16
U8 = mybir.dt.uint8
FP8X4 = mybir.dt.float8_e4m3fn_x4
ALU = mybir.AluOpType
ACT = mybir.ActivationFunctionType

P = 128
PASSES = 2
BLOCKS = 2
NODES = 96
LOG_STEP = -1.0
LOG_FIRST_NODE = 3.25


def tile_picked_yacc_log_p_kernel(tc, x_words, x_scales, hT, gT, offs, tree1, tree2, tree3, out):
    nc = tc.nc
    with ExitStack() as ctx:
        keep = ctx.enter_context(tc.tile_pool(name="keep", bufs=1))
        psum = ctx.enter_context(tc.psum_pool(name="psum", bufs=1))

        scale_table = keep.tile([P, T], U8, name="scale_table")
        nc.gpsimd.memset(scale_table[:].bitcast(I32), 0)

        offs_sb = keep.tile([P, S // 16], U16, name="offs_sb")
        nc.sync.dma_start(offs_sb[:], offs)
        for q in range(4):
            nc.sync.dma_start(
                scale_table[32 * q : 32 * q + 8, :].bitcast(I32),
                x_scales[:, 4 * q : 4 * q + 4, :].bitcast(I32),
            )

        counts = keep.tile([P, NODES], F32, name="counts")
        nc.gpsimd.iota(counts[:], [[1, NODES]], base=0, channel_multiplier=0, allow_small_or_imprecise_dtypes=True)
        nodes = keep.tile([P, NODES], F32, name="nodes")
        nc.scalar.activation(nodes[:], counts[:], ACT.Exp, bias=LOG_FIRST_NODE, scale=-math.exp(LOG_STEP))
        neg_nodes = keep.tile([P, NODES], F32, name="neg_nodes")
        nc.scalar.activation(neg_nodes[:], nodes[:], ACT.Copy, scale=-1.0)

        def load_words(o):
            table = keep.tile([P, T], U32, name=f"word_table{o}", tag=f"word_table{o}", align_bytes=64)
            nc.sync.dma_start(table[:].bitcast(I32), x_words[o].rearrange("p n t -> p (n t)").bitcast(I32))
            return table

        def load_rows(src, name, o, c0, width):
            raw = keep.tile([P, 4, width], F32, name=f"raw_{name}", tag=f"raw_{name}")
            nc.sync.dma_start(raw[:], src[512 * o : 512 * (o + 1), :].rearrange("(p j) c -> p j c", j=4)[:, :, c0 : c0 + width])
            return raw

        def scalar_copy(dst, src):
            nc.scalar.activation(dst, src, ACT.Copy)

        def weave_into(engine_copy, woven, raw):
            engine_copy(woven.rearrange("p (c i) j -> p c j i", i=4), raw.rearrange("p j (c i) -> p c j i", i=4))

        def weave(engine_copy, raw, c0, width, name, tag=None):
            woven = keep.tile([P, width, 4], BF16, name=f"woven_{name}", tag=tag or f"woven_{name}", align_bytes=64)
            engine_copy(
                woven[:].rearrange("p (c i) j -> p c j i", i=4),
                raw[:, :, c0 : c0 + width].rearrange("p j (c i) -> p c j i", i=4),
            )
            return woven

        def quantise(woven, width, name):
            codes = keep.tile([P, width], U32, name=f"codes_{name}", align_bytes=64)
            scales = keep.tile([P, width], U8, name=f"scales_{name}", align_bytes=64)
            nc.vector.quantize_mx(codes[:].bitcast(FP8X4), scales[:], woven.rearrange("p c j -> p (c j)"))
            return codes, scales

        table0 = load_words(0)
        raw_ha = load_rows(hT, "ha", 0, 0, V)
        table1 = load_words(1)
        raw_hb = load_rows(hT, "hb", 1, 0, V)
        raw_ga = load_rows(gT, "ga", 0, 0, V)
        trees = []
        for n, tree in enumerate((tree1, tree2, tree3)):
            tree_sb = keep.tile([P, U // 16], U16, name=f"tree_sb{n}")
            nc.sync.dma_start(tree_sb[:], tree)
            trees.append(tree_sb)
        raw_gb = load_rows(gT, "gb", 1, 0, V)

        picked_words = [keep.tile([P, S], U32, name="picked_words0", align_bytes=64)]
        picked_scales = keep.tile([P, S], U8, name="picked_scales", align_bytes=64)

        def mx_pass(acc, o, codes, scales):
            nc.tensor.matmul_mx(
                acc[:],
                lhsT=codes.bitcast(FP8X4),
                lhsT_scale=scales,
                rhs=picked_words[o][:].bitcast(FP8X4),
                rhs_scale=picked_scales[4 * o :, :],
                start=(o == 0),
                stop=(o == PASSES - 1),
            )


        def column(name):
            return keep.tile([P, 1], F32, name=name)

        def negate(acc, name, tag):
            neg = keep.tile([P, S], F32, name=f"neg_{name}", tag=tag, align_bytes=64)
            neg_max = column(f"neg_max_{name}")
            nc.vector.tensor_scalar(neg[:], acc[:], -1.0, None, ALU.mult, ALU.min, accum_out=neg_max[:])
            return neg, neg_max

        def exp_sum(neg, neg_max, name):
            total = column(f"total_{name}")
            nc.scalar.activation(unused[:], neg[:], ACT.Exp, bias=neg_max[:], scale=-1.0, accum_out=total[:])
            return total

        def neg_log(total, name):
            res = column(f"neg_log_{name}")
            nc.scalar.activation(unused[:, 0:NODES], neg_nodes[:], ACT.Exp, bias=LOG_STEP, scale=total[:], accum_out=res[:])
            return res

        def combine(a, scale, b, name):
            res = column(name)
            nc.scalar.activation(res[:], a[:], ACT.Identity, bias=b[:], scale=scale)
            return res

        def paths(b, gg):
            sums = [keep.tile([P, U], F32, name=f"sum{b}{n}") for n in range(3)]
            halves = [(slice(P * h, P * (h + 1)), slice(8 * h, 8 * (h + 1))) for h in range(2)]
            for part, entries in halves:
                nc.vector.tensor_copy(sums[0][:, part], gg[:].indirect(trees[0][:, entries]))
            for n in (1, 2):
                for part, entries in halves:
                    nc.vector.tensor_tensor(sums[n][:, part], gg[:].indirect(trees[n][:, entries]), sums[n - 1][:, part], ALU.add)
            for part, entries in halves:
                nc.sync.dma_start(out[P * b : P * (b + 1), part], sums[2][:, part])

        y = [psum.tile([P, S], F32, name=f"y{b}") for b in range(BLOCKS)]
        z = [psum.tile([P, S], F32, name=f"z{b}") for b in range(BLOCKS)]
        cols = [slice(P * b, P * (b + 1)) for b in range(BLOCKS)]

        nc.vector.tensor_copy(picked_words[0][:], table0[:].indirect(offs_sb[:]))
        nc.vector.tensor_copy(picked_scales[:], scale_table[:].indirect(offs_sb[:]))
        woven_ha = keep.tile([P, V, 4], BF16, name="woven_ha", tag="woven_ha", align_bytes=64)
        weave_into(nc.vector.tensor_copy, woven_ha[:, 0:P, :], raw_ha[:, :, 0:P])
        weave_into(scalar_copy, woven_ha[:, P:V, :], raw_ha[:, :, P:V])
        codes, scales = quantise(woven_ha[:], V, "ha")
        for b in range(BLOCKS):
            mx_pass(y[b], 0, codes[:, cols[b]], scales[:, cols[b]])
        picked_words.append(keep.tile([P, S], U32, name="picked_words1", tag="woven_ha", align_bytes=64))
        nc.vector.tensor_copy(picked_words[1][:], table1[:].indirect(offs_sb[:]))
        woven_hb = keep.tile([P, V, 4], BF16, name="woven_hb", tag="word_table1", align_bytes=64)
        weave_into(nc.vector.tensor_copy, woven_hb[:, 0:P, :], raw_hb[:, :, 0:P])
        weave_into(scalar_copy, woven_hb[:, P:V, :], raw_hb[:, :, P:V])
        hb_quantised = {b: quantise(woven_hb[:, cols[b], :], P, f"hb{b}") for b in (1, 0)}
        for b in range(BLOCKS):
            mx_pass(y[b], 1, hb_quantised[b][0][:], hb_quantised[b][1][:])
        woven_ga = [weave(scalar_copy, raw_ga, P * b, P, f"ga{b}") for b in range(BLOCKS)]
        ny0, nmy0 = negate(y[0], "y0", "neg_y0")
        for b in range(BLOCKS):
            codes, scales = quantise(woven_ga[b][:], P, f"ga{b}")
            mx_pass(z[b], 0, codes[:], scales[:])
        woven_gb = [weave(nc.vector.tensor_copy, raw_gb, 0, P, "gb0"), weave(scalar_copy, raw_gb, P, P, "gb1")]
        gb_quantised = {b: quantise(woven_gb[b][:], P, f"gb{b}") for b in (1, 0)}
        for b in range(BLOCKS):
            mx_pass(z[b], 1, gb_quantised[b][0][:], gb_quantised[b][1][:])
        unused = keep.tile([P, S], F32, name="unused", tag="raw_gb")
        ny1, nmy1 = negate(y[1], "y1", "woven_gb0")
        nz0, nmz0 = negate(z[0], "z0", "neg_z0")
        ay0 = neg_log(exp_sum(ny0, nmy0, "y0"), "y0")
        sy1 = exp_sum(ny1, nmy1, "y1")
        wy0 = combine(ay0, 1.0, nmy0, "wy0")
        sz0 = exp_sum(nz0, nmz0, "z0")
        ay1 = neg_log(sy1, "y1")
        c0 = combine(wy0, -1.0, neg_log(sz0, "z0"), "c0")
        gg = [keep.tile([P, S], F32, name=f"gg{b}") for b in range(BLOCKS)]
        diffs = [keep.tile([P, S], F32, name=f"diff{b}") for b in range(BLOCKS)]
        nz1, nmz1 = negate(z[1], "z1", "neg_z1")
        nc.vector.scalar_tensor_tensor(diffs[0][:], nz0[:], nmz0[:], ny0[:], ALU.subtract, ALU.subtract)
        nc.vector.scalar_tensor_tensor(diffs[1][:], nz1[:], nmz1[:], ny1[:], ALU.subtract, ALU.subtract)
        sz1 = exp_sum(nz1, nmz1, "z1")
        wy1 = combine(ay1, 1.0, nmy1, "wy1")
        c1 = combine(wy1, -1.0, neg_log(sz1, "z1"), "c1")
        nc.vector.tensor_scalar(gg[0][:], diffs[0][:], c0[:], 0.0, ALU.subtract, ALU.min)
        paths(0, gg[0])
        rejected = keep.tile([P, S], F32, name="rejected")
        nc.scalar.activation(rejected[:], diffs[1][:], ACT.Relu, bias=c1[:], scale=-1.0)
        nc.scalar.activation(gg[1][:], rejected[:], ACT.Copy, scale=-1.0)
        paths(1, gg[1])
